import numpy as np
import ml_dtypes


def mxq(x, axis, fmt="e4m3"):
    dtype, down = {"e4m3": (ml_dtypes.float8_e4m3fn, 7), "e5m2": (ml_dtypes.float8_e5m2, 14)}[fmt]
    v = np.moveaxis(np.asarray(x, np.float32).astype(ml_dtypes.bfloat16).astype(np.float64), axis, -1)
    blocks = v.reshape(v.shape[:-1] + (-1, 32))
    amax = np.abs(blocks).max(-1, keepdims=True)
    byte = np.maximum(np.where(amax > 0, np.frexp(amax)[1] - 1 + 127, 0) - down, 1)
    scale = np.exp2(byte - 127.0)
    codes = (blocks / scale).astype(np.float32).astype(dtype).astype(np.float64)
    return np.moveaxis((codes * scale).reshape(v.shape), -1, axis)


WIDE = False


def mx_kscale(k):
    if not WIDE:
        return np.ones(k)
    levels = np.array([10, -10, 5, -5, 0])
    if k % 512:
        return np.exp2(np.random.permutation(np.resize(levels, k // 32))).repeat(32)
    a = np.empty((k // 512, 16))
    for p in range(k // 512):
        a[p, :8] = np.random.permutation(np.resize(levels, 8))
        for g in range(8):
            far = levels[np.abs(levels - a[p, g]) >= 10]
            a[p, g + 8] = far[np.random.randint(len(far))]
    return np.exp2(a.ravel()).repeat(32)


def f64(x):
    return np.asarray(x).astype(np.float64)


def striped(idx):
    return np.tile(np.asarray(idx).reshape(-1, 16).T, (8, 1)).astype(np.uint16)


def unstriped(offs):
    return offs[:16].T.reshape(-1).astype(np.int64)


B, N, T, D, DV, NQ = 1, 1024, 4096, 512, 128, 256


def setup_inputs():
    n = np.random.standard_normal
    idx = np.random.permutation(T)[:B * N]
    s = mx_kscale(D)[:, None]
    u = np.ones(T)
    u[idx] = mx_kscale(B * N)
    r = np.random.uniform(0.5, 2.0, T)
    k = n((D, T)) / s
    v = n((DV, T)) / (u * r)
    return {
        "qT": (n((B, D, NQ)) * s * (0.80 / np.sqrt(D))).astype(np.float32),
        "kT": k.astype(np.float32),
        "vT": v.astype(np.float32),
        "vs": np.tile(u * r, (128, 1)).astype(np.float32),
        "sink": (2.0 + 3.0 * n((B, NQ, 1))).astype(np.float32),
        "offs": striped(idx),
    }


def reference(qT, kT, vT, vs, sink, offs):
    idx = unstriped(offs)
    k = f64(kT)
    v = f64(vT)
    pick = lambda x: x[:, idx].reshape(x.shape[0], B, N).transpose(1, 0, 2)
    q = f64(qT)
    score = mxq(q, 1, "e4m3").transpose(0, 2, 1) @ mxq(pick(k), 1, "e4m3")
    m = np.maximum(score.max(-1, keepdims=True), f64(sink))
    p = np.exp(score - m)
    total = p.sum(-1, keepdims=True) + np.exp(f64(sink) - m)
    w = p * pick(f64(vs))[:, :1, :]
    y = mxq(w, 2, "e4m3") @ mxq(pick(v).transpose(0, 2, 1), 1, "e4m3")
    y = y / total
    return y

@@ -1,0 +1,214 @@
+from contextlib import ExitStack
+
+import concourse.mybir as mybir
+from concourse.masks import make_identity
+
+D, DV, NQ, T, N = 512, 128, 256, 4096, 1024
+
+FLOPS = 2 * NQ * N * (D + DV)
+BYTES = 4 * (D * T + DV * T + T + D * NQ + NQ + NQ * DV) + 2 * 128 * (N // 16)
+
+F32 = mybir.dt.float32
+BF16 = mybir.dt.bfloat16
+U32 = mybir.dt.uint32
+U16 = mybir.dt.uint16
+U8 = mybir.dt.uint8
+FP8X4 = mybir.dt.float8_e4m3fn_x4
+ALU = mybir.AluOpType
+ACT = mybir.ActivationFunctionType
+AX = mybir.AxisListType
+
+P = 128
+PACK = 4
+HALF = 512
+
+
+def tile_attend_sink_topk_kernel(tc, qT, kT, vT, vs, sink, offs, out):
+    nc = tc.nc
+    with ExitStack() as ctx:
+        lists = ctx.enter_context(tc.tile_pool(name="lists", bufs=1))
+        keep = ctx.enter_context(tc.tile_pool(name="keep", bufs=1))
+        score_banks = ctx.enter_context(tc.psum_pool(name="score_banks", bufs=4))
+        turn_banks = ctx.enter_context(tc.psum_pool(name="turn_banks", bufs=4))
+
+        offsets = lists.tile([P, N // 16], U16, name="offsets")
+        nc.sync.dma_start(offsets[:], offs)
+
+        vs_table = keep.tile([P, T], F32, name="vs_table")
+        nc.vector.memset(vs_table[:], 0.0)
+        sink_raw = keep.tile([P, 2], F32, name="sink_raw")
+        nc.scalar.dma_start(out=sink_raw[:], in_=sink[0].rearrange("(m j) x -> m (j x)", j=2))
+        warm = keep.tile([P, 1], F32, name="warm")
+        nc.gpsimd.memset(warm[:], 0.0)
+        warmed = keep.tile([P, 1], F32, name="warmed")
+        nc.scalar.activation(out=warmed[:], in_=warm[:], func=ACT.Exp)
+
+        k_rows = kT.rearrange("(p t) c -> p t c", t=PACK)
+        k_table = [keep.tile([P, T], F32, name=f"k_table{t}") for t in range(PACK)]
+        for t in range(PACK):
+            nc.sync.dma_start(out=k_table[t][:], in_=k_rows[:, t, :])
+            if t == 0:
+                nc.sync.dma_start(out=vs_table[0:1, :], in_=vs[0:1, :])
+        q_raw = keep.tile([P, PACK, NQ], F32, name="q_raw")
+        nc.sync.dma_start(out=q_raw[:], in_=qT[0].rearrange("(p t) q -> p t q", t=PACK))
+        v_table = keep.tile([P, T], F32, name="v_table")
+        nc.sync.dma_start(out=v_table[:], in_=vT)
+
+        ident = keep.tile([P, P], F32, name="ident")
+        make_identity(nc, ident[:])
+
+        nsink = keep.tile([P, 2], F32, name="nsink")
+        nc.scalar.activation(out=nsink[:], in_=sink_raw[:], func=ACT.Copy, scale=-1.0)
+
+        k_grouped = keep.tile([P, N, PACK], BF16, name="k_grouped", align_bytes=64)
+        nc.vector.tensor_copy(k_grouped[:, :, 0], k_table[0][:].indirect(offsets[:]))
+
+        vs_picked = keep.tile([P, N], F32, name="vs_picked")
+        nc.vector.tensor_copy(vs_picked[:], vs_table[:].indirect(offsets[:]))
+        vcol = keep.tile([P, 2 * PACK], F32, name="vcol")
+        for g in range(2):
+            turned = turn_banks.tile([P, PACK, P], F32, name="turned")
+            for t in range(PACK):
+                nc.tensor.transpose(turned[:, t, :], vs_picked[:, g * HALF + t : (g + 1) * HALF : PACK], ident[:])
+            nc.scalar.copy(out=vcol[:, g * PACK : (g + 1) * PACK], in_=turned[:, :, 0])
+
+        for t in range(1, PACK):
+            nc.vector.tensor_copy(k_grouped[:, :, t], k_table[t][:].indirect(offsets[:]))
+
+        q_grouped = keep.tile([P, NQ, PACK], BF16, name="q_grouped", align_bytes=64)
+        nc.scalar.activation(
+            out=q_grouped[:].rearrange("p (j m) t -> p j m t", j=2),
+            in_=q_raw[:].rearrange("p t (m j) -> p j m t", j=2),
+            func=ACT.Copy,
+            scale=-1.0,
+        )
+        q_codes = keep.tile([P, NQ], U32, name="q_codes", align_bytes=64)
+        q_scales = keep.tile([P, NQ], U8, name="q_scales", align_bytes=64)
+        nc.vector.quantize_mx(out=q_codes[:].bitcast(FP8X4), scales=q_scales[:], in_=q_grouped[:].rearrange("p n t -> p (n t)"))
+
+        k_codes = keep.tile([P, N], U32, name="k_codes", align_bytes=64)
+        k_scales = keep.tile([P, N], U8, name="k_scales", align_bytes=64)
+        scores = {}
+        for h in range(2):
+            cols = slice(h * HALF, (h + 1) * HALF)
+            nc.vector.quantize_mx(
+                out=k_codes[:, cols].bitcast(FP8X4),
+                scales=k_scales[:, cols],
+                in_=k_grouped[:, cols, :].rearrange("p n t -> p (n t)"),
+            )
+            for j in range(2):
+                queries = slice(j * P, (j + 1) * P)
+                scores[j, h] = score_banks.tile([P, HALF], F32, name="score")
+                nc.tensor.matmul_mx(
+                    out=scores[j, h][:],
+                    lhsT=q_codes[:, queries].bitcast(FP8X4),
+                    lhsT_scale=q_scales[:, queries],
+                    rhs=k_codes[:, cols].bitcast(FP8X4),
+                    rhs_scale=k_scales[:, cols],
+                    start=True,
+                    stop=True,
+                )
+
+        low = {}
+        for h in range(2):
+            for j in range(2):
+                unused = keep.tile([P, HALF], F32, name=f"unused{j}{h}")
+                low[j, h] = keep.tile([P, 1], F32, name=f"low{j}{h}")
+                nc.vector.tensor_scalar(
+                    out=unused[:],
+                    in0=scores[j, h][:],
+                    scalar1=1.0,
+                    scalar2=nsink[:, j : j + 1] if h == 0 else low[j, 0][:],
+                    op0=ALU.mult,
+                    op1=ALU.min,
+                    accum_out=low[j, h][:],
+                )
+
+        v_picked = keep.tile([P, N], F32, name="v_picked")
+        v_pairs = keep.tile([P, 2, 2, P, 2], BF16, name="v_pairs")
+        v_turned = turn_banks.tile([P, 2, 2, P], F32, name="turned")
+        v_grouped = keep.tile([P, 2, P, PACK], BF16, name="v_grouped", align_bytes=64)
+        for g in range(2):
+            nc.vector.tensor_copy(
+                v_picked[:, g * HALF : (g + 1) * HALF],
+                v_table[:].indirect(offsets[:, g * (HALF // 16) : (g + 1) * (HALF // 16)]),
+            )
+
+        sums = keep.tile([P, 2, 3], F32, name="sums")
+        probs = {}
+        for j in range(2):
+            for h in range(2):
+                probs[j, h] = keep.tile([P, PACK, P], F32, name=f"probs{j}{h}")
+                nc.scalar.activation(
+                    out=probs[j, h][:],
+                    in_=scores[j, h][:].rearrange("p (s t) -> p t s", t=PACK),
+                    func=ACT.Exp,
+                    bias=low[j, 1][:],
+                    scale=-1.0,
+                    accum_out=sums[:, j, h : h + 1],
+                )
+            nc.scalar.activation(out=sums[:, j, 2:3], in_=nsink[:, j : j + 1], func=ACT.Exp, bias=low[j, 1][:], scale=-1.0)
+
+        for g in range(2):
+            nc.scalar.activation(
+                out=v_pairs[:, g, :, :, :],
+                in_=v_picked[:, g * HALF : (g + 1) * HALF].rearrange("p (s u w) -> p u s w", u=2, w=2),
+                func=ACT.Copy,
+            )
+
+        w_grouped = [keep.tile([P, 2, P, PACK], BF16, name=f"w_grouped{j}", align_bytes=64) for j in range(2)]
+        w_codes = [keep.tile([P, 2, P], U32, name=f"w_codes{j}", align_bytes=64) for j in range(2)]
+        w_scales = [keep.tile([P, 2, P], U8, name=f"w_scales{j}", align_bytes=64) for j in range(2)]
+        v_codes = keep.tile([P, 2, P], U32, name="v_codes", align_bytes=64)
+        v_scales = keep.tile([P, 2, P], U8, name="v_scales", align_bytes=64)
+        total = keep.tile([P, 2], F32, name="total")
+        share = keep.tile([P, 2], F32, name="share")
+
+        for j in range(2):
+            for g in range(2):
+                turned = turn_banks.tile([P, PACK, P], F32, name="turned")
+                for t in range(PACK):
+                    nc.tensor.transpose(turned[:, t, :], probs[j, g][:, t, :], ident[:])
+                nc.vector.tensor_tensor(
+                    w_grouped[j][:, g, :, :],
+                    turned[:].rearrange("p t q -> p q t"),
+                    vcol[:, g * PACK : (g + 1) * PACK].unsqueeze(1).to_broadcast([P, P, PACK]),
+                    ALU.mult,
+                )
+            if j == 0:
+                v_words = v_pairs[:].rearrange("p g u s w -> p (g u s w)").bitcast(F32)
+                for g in range(2):
+                    for u in range(2):
+                        first = (2 * g + u) * P
+                        nc.tensor.transpose(v_turned[:, g, u, :], v_words[:, first : first + P], ident[:])
+                nc.scalar.copy(
+                    out=v_grouped[:].rearrange("p g e t -> p (g e t)").bitcast(F32).rearrange("p (g e u) -> p g e u", g=2, u=2),
+                    in_=v_turned[:].rearrange("p g u e -> p g e u"),
+                )
+            nc.vector.quantize_mx(
+                out=w_codes[j][:].rearrange("p g q -> p (g q)").bitcast(FP8X4),
+                scales=w_scales[j][:].rearrange("p g q -> p (g q)"),
+                in_=w_grouped[j][:].rearrange("p g q t -> p (g q t)"),
+            )
+            if j == 0:
+                nc.vector.quantize_mx(
+                    out=v_codes[:].rearrange("p g e -> p (g e)").bitcast(FP8X4),
+                    scales=v_scales[:].rearrange("p g e -> p (g e)"),
+                    in_=v_grouped[:].rearrange("p g e t -> p (g e t)"),
+                )
+                nc.vector.tensor_reduce(out=total[:], in_=sums[:], axis=AX.X, op=ALU.add)
+                nc.vector.reciprocal(share[:], total[:])
+            acc = score_banks.tile([P, DV], F32, name="score")
+            for g in range(2):
+                nc.tensor.matmul_mx(
+                    out=acc[:],
+                    lhsT=w_codes[j][:, g, :].bitcast(FP8X4),
+                    lhsT_scale=w_scales[j][:, g, :],
+                    rhs=v_codes[:, g, :].bitcast(FP8X4),
+                    rhs_scale=v_scales[:, g, :],
+                    start=(g == 0),
+                    stop=(g == 1),
+                )
+            result = keep.tile([P, DV], F32, name=f"result{j}")
+            nc.scalar.activation(out=result[:], in_=acc[:], func=ACT.Copy, scale=share[:, j : j + 1])
+            nc.sync.dma_start(out=out[0].rearrange("(m j) e -> m j e", j=2)[:, j, :], in_=result[:])

@@ -60,8 +60,10 @@ def tile_attend_sink_topk_kernel(tc, qT, kT, vT, vs, sink, offs, out):
         nsink = keep.tile([P, 2], F32, name="nsink")
         nc.scalar.activation(out=nsink[:], in_=sink_raw[:], func=ACT.Copy, scale=-1.0)
 
-        k_grouped = keep.tile([P, N, PACK], BF16, name="k_grouped", align_bytes=64)
-        nc.vector.tensor_copy(k_grouped[:, :, 0], k_table[0][:].indirect(offsets[:]))
+        k_grouped = [keep.tile([P, HALF, PACK], BF16, name=f"k_grouped{h}", align_bytes=64) for h in range(2)]
+        k_low = keep.tile([P, 2, N], F32, name="k_low")
+        k_high = keep.tile([P, 2, HALF], F32, name="k_high")
+        nc.vector.tensor_copy(k_low[:, 0, :], k_table[0][:].indirect(offsets[:]))
 
         vs_picked = keep.tile([P, N], F32, name="vs_picked")
         nc.vector.tensor_copy(vs_picked[:], vs_table[:].indirect(offsets[:]))
@@ -72,30 +74,42 @@ def tile_attend_sink_topk_kernel(tc, qT, kT, vT, vs, sink, offs, out):
                 nc.tensor.transpose(turned[:, t, :], vs_picked[:, g * HALF + t : (g + 1) * HALF : PACK], ident[:])
             nc.scalar.copy(out=vcol[:, g * PACK : (g + 1) * PACK], in_=turned[:, :, 0])
 
-        for t in range(1, PACK):
-            nc.vector.tensor_copy(k_grouped[:, :, t], k_table[t][:].indirect(offsets[:]))
+        nc.vector.tensor_copy(k_low[:, 1, :], k_table[1][:].indirect(offsets[:]))
+        for h in (1, 0):
+            nc.scalar.activation(
+                out=k_grouped[h][:, :, 0:2], in_=k_low[:, :, h * HALF : (h + 1) * HALF].rearrange("p t n -> p n t"), func=ACT.Copy
+            )
+        for t in (2, 3):
+            nc.vector.tensor_copy(k_high[:, t - 2, :], k_table[t][:].indirect(offsets[:, 0 : HALF // 16]))
+            nc.vector.tensor_copy(k_grouped[1][:, :, t], k_table[t][:].indirect(offsets[:, HALF // 16 : N // 16]))
+        nc.scalar.activation(out=k_grouped[0][:, :, 2:4], in_=k_high[:].rearrange("p t n -> p n t"), func=ACT.Copy)
 
         q_grouped = keep.tile([P, NQ, PACK], BF16, name="q_grouped", align_bytes=64)
-        nc.scalar.activation(
+        nc.gpsimd.tensor_scalar(
             out=q_grouped[:].rearrange("p (j m) t -> p j m t", j=2),
-            in_=q_raw[:].rearrange("p t (m j) -> p j m t", j=2),
-            func=ACT.Copy,
-            scale=-1.0,
+            in0=q_raw[:].rearrange("p t (m j) -> p j m t", j=2),
+            scalar1=-1.0,
+            scalar2=0.0,
+            op0=ALU.mult,
+            op1=ALU.add,
         )
         q_codes = keep.tile([P, NQ], U32, name="q_codes", align_bytes=64)
         q_scales = keep.tile([P, NQ], U8, name="q_scales", align_bytes=64)
-        nc.vector.quantize_mx(out=q_codes[:].bitcast(FP8X4), scales=q_scales[:], in_=q_grouped[:].rearrange("p n t -> p (n t)"))
 
         k_codes = keep.tile([P, N], U32, name="k_codes", align_bytes=64)
         k_scales = keep.tile([P, N], U8, name="k_scales", align_bytes=64)
         scores = {}
-        for h in range(2):
+        for h in (1, 0):
             cols = slice(h * HALF, (h + 1) * HALF)
             nc.vector.quantize_mx(
                 out=k_codes[:, cols].bitcast(FP8X4),
                 scales=k_scales[:, cols],
-                in_=k_grouped[:, cols, :].rearrange("p n t -> p (n t)"),
+                in_=k_grouped[h][:].rearrange("p n t -> p (n t)"),
             )
+            if h == 1:
+                nc.vector.quantize_mx(
+                    out=q_codes[:].bitcast(FP8X4), scales=q_scales[:], in_=q_grouped[:].rearrange("p n t -> p (n t)")
+                )
             for j in range(2):
                 queries = slice(j * P, (j + 1) * P)
                 scores[j, h] = score_banks.tile([P, HALF], F32, name="score")
@@ -110,7 +124,7 @@ def tile_attend_sink_topk_kernel(tc, qT, kT, vT, vs, sink, offs, out):
                 )
 
         low = {}
-        for h in range(2):
+        for h in (1, 0):
             for j in range(2):
                 unused = keep.tile([P, HALF], F32, name=f"unused{j}{h}")
                 low[j, h] = keep.tile([P, 1], F32, name=f"low{j}{h}")
@@ -118,15 +132,13 @@ def tile_attend_sink_topk_kernel(tc, qT, kT, vT, vs, sink, offs, out):
                     out=unused[:],
                     in0=scores[j, h][:],
                     scalar1=1.0,
-                    scalar2=nsink[:, j : j + 1] if h == 0 else low[j, 0][:],
+                    scalar2=nsink[:, j : j + 1] if h == 1 else low[j, 1][:],
                     op0=ALU.mult,
                     op1=ALU.min,
                     accum_out=low[j, h][:],
                 )
 
         v_picked = keep.tile([P, N], F32, name="v_picked")
-        v_pairs = keep.tile([P, 2, 2, P, 2], BF16, name="v_pairs")
-        v_turned = turn_banks.tile([P, 2, 2, P], F32, name="turned")
         v_grouped = keep.tile([P, 2, P, PACK], BF16, name="v_grouped", align_bytes=64)
         for g in range(2):
             nc.vector.tensor_copy(
@@ -143,18 +155,12 @@ def tile_attend_sink_topk_kernel(tc, qT, kT, vT, vs, sink, offs, out):
                     out=probs[j, h][:],
                     in_=scores[j, h][:].rearrange("p (s t) -> p t s", t=PACK),
                     func=ACT.Exp,
-                    bias=low[j, 1][:],
+                    bias=low[j, 0][:],
                     scale=-1.0,
                     accum_out=sums[:, j, h : h + 1],
                 )
-            nc.scalar.activation(out=sums[:, j, 2:3], in_=nsink[:, j : j + 1], func=ACT.Exp, bias=low[j, 1][:], scale=-1.0)
-
-        for g in range(2):
-            nc.scalar.activation(
-                out=v_pairs[:, g, :, :, :],
-                in_=v_picked[:, g * HALF : (g + 1) * HALF].rearrange("p (s u w) -> p u s w", u=2, w=2),
-                func=ACT.Copy,
-            )
+        for j in range(2):
+            nc.scalar.activation(out=sums[:, j, 2:3], in_=nsink[:, j : j + 1], func=ACT.Exp, bias=low[j, 0][:], scale=-1.0)
 
         w_grouped = [keep.tile([P, 2, P, PACK], BF16, name=f"w_grouped{j}", align_bytes=64) for j in range(2)]
         w_codes = [keep.tile([P, 2, P], U32, name=f"w_codes{j}", align_bytes=64) for j in range(2)]
@@ -176,15 +182,11 @@ def tile_attend_sink_topk_kernel(tc, qT, kT, vT, vs, sink, offs, out):
                     ALU.mult,
                 )
             if j == 0:
-                v_words = v_pairs[:].rearrange("p g u s w -> p (g u s w)").bitcast(F32)
                 for g in range(2):
-                    for u in range(2):
-                        first = (2 * g + u) * P
-                        nc.tensor.transpose(v_turned[:, g, u, :], v_words[:, first : first + P], ident[:])
-                nc.scalar.copy(
-                    out=v_grouped[:].rearrange("p g e t -> p (g e t)").bitcast(F32).rearrange("p (g e u) -> p g e u", g=2, u=2),
-                    in_=v_turned[:].rearrange("p g u e -> p g e u"),
-                )
+                    v_turned = turn_banks.tile([P, PACK, P], F32, name="turned")
+                    for t in range(PACK):
+                        nc.tensor.transpose(v_turned[:, t, :], v_picked[:, g * HALF + t : (g + 1) * HALF : PACK], ident[:])
+                    nc.scalar.copy(out=v_grouped[:, g, :, :], in_=v_turned[:].rearrange("p t e -> p e t"))
             nc.vector.quantize_mx(
                 out=w_codes[j][:].rearrange("p g q -> p (g q)").bitcast(FP8X4),
                 scales=w_scales[j][:].rearrange("p g q -> p (g q)"),

from contextlib import ExitStack

import concourse.mybir as mybir
from concourse.masks import make_identity

D, DV, NQ, T, N = 512, 128, 256, 4096, 1024

FLOPS = 2 * NQ * N * (D + DV)
BYTES = 4 * (D * T + DV * T + T + D * NQ + NQ + NQ * DV) + 2 * 128 * (N // 16)

F32 = mybir.dt.float32
BF16 = mybir.dt.bfloat16
U32 = mybir.dt.uint32
U16 = mybir.dt.uint16
U8 = mybir.dt.uint8
FP8X4 = mybir.dt.float8_e4m3fn_x4
ALU = mybir.AluOpType
ACT = mybir.ActivationFunctionType
AX = mybir.AxisListType

P = 128
PACK = 4
HALF = 512


def tile_attend_sink_topk_kernel(tc, qT, kT, vT, vs, sink, offs, out):
    nc = tc.nc
    with ExitStack() as ctx:
        lists = ctx.enter_context(tc.tile_pool(name="lists", bufs=1))
        keep = ctx.enter_context(tc.tile_pool(name="keep", bufs=1))
        score_banks = ctx.enter_context(tc.psum_pool(name="score_banks", bufs=4))
        turn_banks = ctx.enter_context(tc.psum_pool(name="turn_banks", bufs=4))

        offsets = lists.tile([P, N // 16], U16, name="offsets")
        nc.sync.dma_start(offsets[:], offs)

        vs_table = keep.tile([P, T], F32, name="vs_table")
        nc.vector.memset(vs_table[:], 0.0)
        sink_raw = keep.tile([P, 2], F32, name="sink_raw")
        nc.scalar.dma_start(out=sink_raw[:], in_=sink[0].rearrange("(m j) x -> m (j x)", j=2))
        warm = keep.tile([P, 1], F32, name="warm")
        nc.gpsimd.memset(warm[:], 0.0)
        warmed = keep.tile([P, 1], F32, name="warmed")
        nc.scalar.activation(out=warmed[:], in_=warm[:], func=ACT.Exp)

        k_rows = kT.rearrange("(p t) c -> p t c", t=PACK)
        k_table = [keep.tile([P, T], F32, name=f"k_table{t}") for t in range(PACK)]
        for t in range(PACK):
            nc.sync.dma_start(out=k_table[t][:], in_=k_rows[:, t, :])
            if t == 0:
                nc.sync.dma_start(out=vs_table[0:1, :], in_=vs[0:1, :])
        q_raw = keep.tile([P, PACK, NQ], F32, name="q_raw")
        nc.sync.dma_start(out=q_raw[:], in_=qT[0].rearrange("(p t) q -> p t q", t=PACK))
        v_table = keep.tile([P, T], F32, name="v_table")
        nc.sync.dma_start(out=v_table[:], in_=vT)

        ident = keep.tile([P, P], F32, name="ident")
        make_identity(nc, ident[:])

        nsink = keep.tile([P, 2], F32, name="nsink")
        nc.scalar.activation(out=nsink[:], in_=sink_raw[:], func=ACT.Copy, scale=-1.0)

        k_grouped = [keep.tile([P, HALF, PACK], BF16, name=f"k_grouped{h}", align_bytes=64) for h in range(2)]
        k_low = keep.tile([P, 2, N], F32, name="k_low")
        k_high = keep.tile([P, 2, HALF], F32, name="k_high")
        nc.vector.tensor_copy(k_low[:, 0, :], k_table[0][:].indirect(offsets[:]))

        vs_picked = keep.tile([P, N], F32, name="vs_picked")
        nc.vector.tensor_copy(vs_picked[:], vs_table[:].indirect(offsets[:]))
        vcol = keep.tile([P, 2 * PACK], F32, name="vcol")
        for g in range(2):
            turned = turn_banks.tile([P, PACK, P], F32, name="turned")
            for t in range(PACK):
                nc.tensor.transpose(turned[:, t, :], vs_picked[:, g * HALF + t : (g + 1) * HALF : PACK], ident[:])
            nc.scalar.copy(out=vcol[:, g * PACK : (g + 1) * PACK], in_=turned[:, :, 0])

        nc.vector.tensor_copy(k_low[:, 1, :], k_table[1][:].indirect(offsets[:]))
        for h in (1, 0):
            nc.scalar.activation(
                out=k_grouped[h][:, :, 0:2], in_=k_low[:, :, h * HALF : (h + 1) * HALF].rearrange("p t n -> p n t"), func=ACT.Copy
            )
        for t in (2, 3):
            nc.vector.tensor_copy(k_high[:, t - 2, :], k_table[t][:].indirect(offsets[:, 0 : HALF // 16]))
            nc.vector.tensor_copy(k_grouped[1][:, :, t], k_table[t][:].indirect(offsets[:, HALF // 16 : N // 16]))
        nc.scalar.activation(out=k_grouped[0][:, :, 2:4], in_=k_high[:].rearrange("p t n -> p n t"), func=ACT.Copy)

        q_grouped = keep.tile([P, NQ, PACK], BF16, name="q_grouped", align_bytes=64)
        nc.gpsimd.tensor_scalar(
            out=q_grouped[:].rearrange("p (j m) t -> p j m t", j=2),
            in0=q_raw[:].rearrange("p t (m j) -> p j m t", j=2),
            scalar1=-1.0,
            scalar2=0.0,
            op0=ALU.mult,
            op1=ALU.add,
        )
        q_codes = keep.tile([P, NQ], U32, name="q_codes", align_bytes=64)
        q_scales = keep.tile([P, NQ], U8, name="q_scales", align_bytes=64)

        k_codes = keep.tile([P, N], U32, name="k_codes", align_bytes=64)
        k_scales = keep.tile([P, N], U8, name="k_scales", align_bytes=64)
        scores = {}
        for h in (1, 0):
            cols = slice(h * HALF, (h + 1) * HALF)
            nc.vector.quantize_mx(
                out=k_codes[:, cols].bitcast(FP8X4),
                scales=k_scales[:, cols],
                in_=k_grouped[h][:].rearrange("p n t -> p (n t)"),
            )
            if h == 1:
                nc.vector.quantize_mx(
                    out=q_codes[:].bitcast(FP8X4), scales=q_scales[:], in_=q_grouped[:].rearrange("p n t -> p (n t)")
                )
            for j in range(2):
                queries = slice(j * P, (j + 1) * P)
                scores[j, h] = score_banks.tile([P, HALF], F32, name="score")
                nc.tensor.matmul_mx(
                    out=scores[j, h][:],
                    lhsT=q_codes[:, queries].bitcast(FP8X4),
                    lhsT_scale=q_scales[:, queries],
                    rhs=k_codes[:, cols].bitcast(FP8X4),
                    rhs_scale=k_scales[:, cols],
                    start=True,
                    stop=True,
                )

        low = {}
        for h in (1, 0):
            for j in range(2):
                unused = keep.tile([P, HALF], F32, name=f"unused{j}{h}")
                low[j, h] = keep.tile([P, 1], F32, name=f"low{j}{h}")
                nc.vector.tensor_scalar(
                    out=unused[:],
                    in0=scores[j, h][:],
                    scalar1=1.0,
                    scalar2=nsink[:, j : j + 1] if h == 1 else low[j, 1][:],
                    op0=ALU.mult,
                    op1=ALU.min,
                    accum_out=low[j, h][:],
                )

        v_picked = keep.tile([P, N], F32, name="v_picked")
        v_grouped = keep.tile([P, 2, P, PACK], BF16, name="v_grouped", align_bytes=64)
        for g in range(2):
            nc.vector.tensor_copy(
                v_picked[:, g * HALF : (g + 1) * HALF],
                v_table[:].indirect(offsets[:, g * (HALF // 16) : (g + 1) * (HALF // 16)]),
            )

        sums = keep.tile([P, 2, 3], F32, name="sums")
        probs = {}
        for j in range(2):
            for h in range(2):
                probs[j, h] = keep.tile([P, PACK, P], F32, name=f"probs{j}{h}")
                nc.scalar.activation(
                    out=probs[j, h][:],
                    in_=scores[j, h][:].rearrange("p (s t) -> p t s", t=PACK),
                    func=ACT.Exp,
                    bias=low[j, 0][:],
                    scale=-1.0,
                    accum_out=sums[:, j, h : h + 1],
                )
        for j in range(2):
            nc.scalar.activation(out=sums[:, j, 2:3], in_=nsink[:, j : j + 1], func=ACT.Exp, bias=low[j, 0][:], scale=-1.0)

        w_grouped = [keep.tile([P, 2, P, PACK], BF16, name=f"w_grouped{j}", align_bytes=64) for j in range(2)]
        w_codes = [keep.tile([P, 2, P], U32, name=f"w_codes{j}", align_bytes=64) for j in range(2)]
        w_scales = [keep.tile([P, 2, P], U8, name=f"w_scales{j}", align_bytes=64) for j in range(2)]
        v_codes = keep.tile([P, 2, P], U32, name="v_codes", align_bytes=64)
        v_scales = keep.tile([P, 2, P], U8, name="v_scales", align_bytes=64)
        total = keep.tile([P, 2], F32, name="total")
        share = keep.tile([P, 2], F32, name="share")

        for j in range(2):
            for g in range(2):
                turned = turn_banks.tile([P, PACK, P], F32, name="turned")
                for t in range(PACK):
                    nc.tensor.transpose(turned[:, t, :], probs[j, g][:, t, :], ident[:])
                nc.vector.tensor_tensor(
                    w_grouped[j][:, g, :, :],
                    turned[:].rearrange("p t q -> p q t"),
                    vcol[:, g * PACK : (g + 1) * PACK].unsqueeze(1).to_broadcast([P, P, PACK]),
                    ALU.mult,
                )
            if j == 0:
                for g in range(2):
                    v_turned = turn_banks.tile([P, PACK, P], F32, name="turned")
                    for t in range(PACK):
                        nc.tensor.transpose(v_turned[:, t, :], v_picked[:, g * HALF + t : (g + 1) * HALF : PACK], ident[:])
                    nc.scalar.copy(out=v_grouped[:, g, :, :], in_=v_turned[:].rearrange("p t e -> p e t"))
            nc.vector.quantize_mx(
                out=w_codes[j][:].rearrange("p g q -> p (g q)").bitcast(FP8X4),
                scales=w_scales[j][:].rearrange("p g q -> p (g q)"),
                in_=w_grouped[j][:].rearrange("p g q t -> p (g q t)"),
            )
            if j == 0:
                nc.vector.quantize_mx(
                    out=v_codes[:].rearrange("p g e -> p (g e)").bitcast(FP8X4),
                    scales=v_scales[:].rearrange("p g e -> p (g e)"),
                    in_=v_grouped[:].rearrange("p g e t -> p (g e t)"),
                )
                nc.vector.tensor_reduce(out=total[:], in_=sums[:], axis=AX.X, op=ALU.add)
                nc.vector.reciprocal(share[:], total[:])
            acc = score_banks.tile([P, DV], F32, name="score")
            for g in range(2):
                nc.tensor.matmul_mx(
                    out=acc[:],
                    lhsT=w_codes[j][:, g, :].bitcast(FP8X4),
                    lhsT_scale=w_scales[j][:, g, :],
                    rhs=v_codes[:, g, :].bitcast(FP8X4),
                    rhs_scale=v_scales[:, g, :],
                    start=(g == 0),
                    stop=(g == 1),
                )
            result = keep.tile([P, DV], F32, name=f"result{j}")
            nc.scalar.activation(out=result[:], in_=acc[:], func=ACT.Copy, scale=share[:, j : j + 1])
            nc.sync.dma_start(out=out[0].rearrange("(m j) e -> m j e", j=2)[:, j, :], in_=result[:])
